import numpy as np
import ml_dtypes


def mxq(x, axis, fmt="e4m3"):
    dtype, down = {"e4m3": (ml_dtypes.float8_e4m3fn, 7), "e5m2": (ml_dtypes.float8_e5m2, 14)}[fmt]
    v = np.moveaxis(np.asarray(x, np.float32).astype(ml_dtypes.bfloat16).astype(np.float64), axis, -1)
    blocks = v.reshape(v.shape[:-1] + (-1, 32))
    amax = np.abs(blocks).max(-1, keepdims=True)
    byte = np.maximum(np.where(amax > 0, np.frexp(amax)[1] - 1 + 127, 0) - down, 1)
    scale = np.exp2(byte - 127.0)
    codes = (blocks / scale).astype(np.float32).astype(dtype).astype(np.float64)
    return np.moveaxis((codes * scale).reshape(v.shape), -1, axis)


WIDE = False


def mx_kscale(k):
    if not WIDE:
        return np.ones(k)
    levels = np.array([10, -10, 5, -5, 0])
    if k % 512:
        return np.exp2(np.random.permutation(np.resize(levels, k // 32))).repeat(32)
    a = np.empty((k // 512, 16))
    for p in range(k // 512):
        a[p, :8] = np.random.permutation(np.resize(levels, 8))
        for g in range(8):
            far = levels[np.abs(levels - a[p, g]) >= 10]
            a[p, g + 8] = far[np.random.randint(len(far))]
    return np.exp2(a.ravel()).repeat(32)


def f64(x):
    return np.asarray(x).astype(np.float64)


def striped(idx):
    return np.tile(idx.reshape(-1, 16).T, (8, 1)).astype(np.uint16)


def unstriped(offs):
    return offs[:16].T.reshape(-1).astype(np.int64)


def pack_weight(w):
    k, n = w.shape
    w = f64(np.asarray(w, np.float32).astype(ml_dtypes.bfloat16)).reshape(k // 32, 32, n)
    amax = np.abs(w).max(1)
    byte = np.clip(np.where(amax > 0, np.frexp(amax)[1] - 1 + 127 - 7, 1), 1, 254)
    scaled = (w * np.exp2(127.0 - byte)[:, None, :]).reshape(k, n).astype(np.float32)
    words = np.ascontiguousarray(scaled.reshape(k // 512, 128, 4, n).transpose(0, 1, 3, 2)).astype(ml_dtypes.float8_e4m3fn).view(np.uint8)
    return words, np.ascontiguousarray(byte.astype(np.uint8).reshape(k // 512, 16, n))


def unpack_weight(words, scales):
    g, p, n, _ = words.shape
    vals = np.ascontiguousarray(words).view(ml_dtypes.float8_e4m3fn).astype(np.float64) * np.repeat(np.exp2(scales.astype(np.float64) - 127.0), 8, axis=1)[..., None]
    return vals.transpose(0, 1, 3, 2).reshape(g * 512, n)


K, T, S, N, U = 1024, 1024, 512, 128, 1024


def setup_inputs():
    n = np.random.standard_normal
    s = mx_kscale(K)[:, None]
    packed_xT = pack_weight(n((K, T)) * s)
    return {
        "x_words": packed_xT[0],
        "x_scales": packed_xT[1],
        "w1": (n((K, N)) / np.sqrt(K) / s).astype(np.float32),
        "cnt0": (np.random.uniform(0.0, 4.0, (N, U))).astype(np.float32),
        "cnt1": (np.random.uniform(0.0, 4.0, (N, U))).astype(np.float32),
        "cnt2": (np.random.uniform(0.0, 4.0, (N, U))).astype(np.float32),
        "offs": striped(np.random.permutation(T)[:S]),
        "hash0": striped(np.random.permutation(U)[:S]),
        "hash1": striped(np.random.permutation(U)[:S]),
        "hash2": striped(np.random.permutation(U)[:S]),
    }


def reference(x_words, x_scales, w1, cnt0, cnt1, cnt2, offs, hash0, hash1, hash2):
    xq = unpack_weight(x_words, x_scales)[:, unstriped(offs)]
    y = mxq(f64(w1), 0, "e4m3").T @ xq
    inc = np.log(np.exp(y) + 1.0)
    g0 = f64(cnt0)[:, unstriped(hash0)]
    g1 = f64(cnt1)[:, unstriped(hash1)]
    g2 = f64(cnt2)[:, unstriped(hash2)]
    est = np.minimum(np.minimum(g0, g1), g2) + inc
    return inc / est + 0.3 * (np.log((np.maximum(np.maximum(g0, g1), g2) + 0.2) / (est - inc + 0.2)))

@@ -1,0 +1,143 @@
+from contextlib import ExitStack
+
+import concourse.mybir as mybir
+
+K, T, S, N, U = 1024, 1024, 512, 128, 1024
+FLOPS = 2 * K * S * N
+
+F32 = mybir.dt.float32
+BF16 = mybir.dt.bfloat16
+I32 = mybir.dt.int32
+U32 = mybir.dt.uint32
+U16 = mybir.dt.uint16
+U8 = mybir.dt.uint8
+FP8X4 = mybir.dt.float8_e4m3fn_x4
+ALU = mybir.AluOpType
+ACT = mybir.ActivationFunctionType
+
+P = 128
+PASSES = 2
+HALF = S // 2
+TINY_INC = 2.0 ** -44
+TINY_MIN = 2.0 ** -63
+
+
+def tile_picked_ycms2_share_p_kernel(
+    tc, x_words, x_scales, w1, cnt0, cnt1, cnt2, offs, hash0, hash1, hash2, out
+):
+    nc = tc.nc
+    with ExitStack() as ctx:
+        keep = ctx.enter_context(tc.tile_pool(name="keep", bufs=1))
+        psum = ctx.enter_context(tc.psum_pool(name="psum", bufs=1))
+
+        def f32(name, width=S):
+            return keep.tile([P, width], F32, name=name, tag=name, align_bytes=64)
+
+        halves = [slice(h * HALF, (h + 1) * HALF) for h in range(2)]
+
+        scale_table = keep.tile([P, T], U8, name="scale_table", align_bytes=64)
+        nc.vector.memset(scale_table[:].bitcast(I32), 0)
+
+        word_table = [keep.tile([P, T], I32, name=f"word_table{g}", align_bytes=64) for g in range(PASSES)]
+        lists = [keep.tile([P, S // 16], U16, name=f"list{i}") for i in range(4)]
+        counters = [f32(f"counters{i}", U) for i in range(3)]
+        w_raw = keep.tile([P, PASSES, 4, N], F32, name="w_raw", align_bytes=64)
+
+        def load_words(g):
+            nc.sync.dma_start(word_table[g][:], x_words[g].rearrange("p c r -> p (c r)").bitcast(I32))
+
+        load_words(0)
+        nc.sync.dma_start(lists[0][:], offs)
+        for q in range(4):
+            nc.sync.dma_start(
+                scale_table[32 * q : 32 * q + 8, :].bitcast(I32),
+                x_scales[:, 4 * q : 4 * q + 4, :].bitcast(I32),
+            )
+        nc.sync.dma_start(w_raw[:], w1.rearrange("(g p j) n -> p g j n", g=PASSES, j=4))
+        load_words(1)
+        for i, (table, hashes) in enumerate(((cnt0, hash0), (cnt1, hash1), (cnt2, hash2))):
+            nc.sync.dma_start(lists[1 + i][:], hashes)
+            nc.sync.dma_start(counters[i][:], table)
+
+        w_bf = [keep.tile([P, N, 4], BF16, name=f"w_bf{g}", tag=f"w_bf{g}", align_bytes=64) for g in range(PASSES)]
+        for g in range(PASSES):
+            nc.scalar.activation(w_bf[g][:], w_raw[:, g].rearrange("p j n -> p n j"), ACT.Copy)
+
+        words0 = keep.tile([P, S], U32, name="words0", align_bytes=64)
+        nc.vector.tensor_copy(words0[:], word_table[0][:].bitcast(U32).indirect(lists[0][:]))
+        scales = keep.tile([P, S], U8, name="scales", align_bytes=64)
+        nc.vector.tensor_copy(scales[:], scale_table[:].indirect(lists[0][:]))
+
+        w_codes = keep.tile([P, PASSES * N], U32, name="w_codes", align_bytes=64)
+        w_scales = keep.tile([P, PASSES * N], U8, name="w_scales", align_bytes=64)
+        words1 = []
+        for g in range(PASSES):
+            nc.vector.quantize_mx(
+                out=w_codes[:, g * N : (g + 1) * N].bitcast(FP8X4),
+                scales=w_scales[:, g * N : (g + 1) * N],
+                in_=w_bf[g][:].rearrange("p n j -> p (n j)"),
+            )
+            words1.append(keep.tile([P, HALF], U32, name=f"words1_{g}", tag=f"w_bf{g}", align_bytes=64))
+            nc.vector.tensor_copy(
+                words1[g][:], word_table[1][:].bitcast(U32).indirect(lists[0][:, 16 * g : 16 * (g + 1)])
+            )
+
+        y = [psum.tile([P, HALF], F32, name=f"y{h}") for h in range(2)]
+        for g in range(PASSES):
+            for h in range(2):
+                moving = words0[:, halves[h]] if g == 0 else words1[h][:]
+                nc.tensor.matmul_mx(
+                    out=y[h][:],
+                    lhsT=w_codes[:, g * N : (g + 1) * N].bitcast(FP8X4),
+                    lhsT_scale=w_scales[:, g * N : (g + 1) * N],
+                    rhs=moving.bitcast(FP8X4),
+                    rhs_scale=scales[4 * g : P, halves[h]],
+                    start=(g == 0),
+                    stop=(g == PASSES - 1),
+                )
+
+        y_abs = f32("y_abs")
+        decay = f32("decay")
+        for h in range(2):
+            nc.scalar.activation(y_abs[:, halves[h]], y[h][:], ACT.Abs)
+            nc.scalar.activation(decay[:, halves[h]], y_abs[:, halves[h]], ACT.Exp, scale=-1.0)
+        log1p = f32("log1p")
+        for h in range(2):
+            nc.scalar.activation(log1p[:, halves[h]], decay[:, halves[h]], ACT.Ln, bias=1.0)
+
+        picked = [f32(f"picked{i}") for i in range(3)]
+        for i in range(3):
+            nc.vector.tensor_copy(picked[i][:], counters[i][:].indirect(lists[1 + i][:]))
+
+        late = keep.tile([P, 3 * S], F32, name="late", tag="counters2", align_bytes=64)
+        low01, inc, high01 = (late[:, i * S : (i + 1) * S] for i in range(3))
+        low, high = f32("low"), f32("high")
+        nc.vector.tensor_tensor(low01[:], picked[0][:], picked[1][:], ALU.min)
+        for h in range(2):
+            nc.vector.scalar_tensor_tensor(
+                inc[:, halves[h]], y[h][:], 0.0, log1p[:, halves[h]], ALU.max, ALU.add
+            )
+        nc.vector.tensor_tensor(low[:], low01[:], picked[2][:], ALU.min)
+        for h in range(2):
+            nc.vector.tensor_tensor(high01[:, halves[h]], picked[0][:, halves[h]], picked[1][:, halves[h]], ALU.max)
+        for h in range(2):
+            nc.vector.tensor_tensor(high[:, halves[h]], high01[:, halves[h]], picked[2][:, halves[h]], ALU.max)
+
+        ln_inc, ln_low, ln_low2, ln_high2 = (f32(n) for n in ("ln_inc", "ln_low", "ln_low2", "ln_high2"))
+        nc.scalar.activation(ln_inc[:], inc[:], ACT.Ln, bias=TINY_INC)
+        nc.scalar.activation(ln_low[:], low[:], ACT.Ln, bias=TINY_MIN)
+        nc.scalar.activation(ln_low2[:], low[:], ACT.Ln, bias=0.2)
+        for h in range(2):
+            nc.scalar.activation(ln_high2[:, halves[h]], high[:, halves[h]], ACT.Ln, bias=0.2)
+
+        spread, share, result = (f32(n) for n in ("spread", "share", "result"))
+        logit = high
+        nc.vector.tensor_tensor(logit[:], ln_inc[:], ln_low[:], ALU.subtract)
+        nc.vector.tensor_tensor(spread[:], ln_high2[:], ln_low2[:], ALU.subtract)
+        for h in range(2):
+            nc.scalar.activation(share[:, halves[h]], logit[:, halves[h]], ACT.Sigmoid)
+        for h in range(2):
+            nc.vector.scalar_tensor_tensor(
+                result[:, halves[h]], spread[:, halves[h]], 0.3, share[:, halves[h]], ALU.mult, ALU.add
+            )
+            nc.sync.dma_start(out[:, halves[h]], result[:, halves[h]])

@@ -28,10 +28,14 @@ def tile_picked_ycms2_share_p_kernel(
     nc = tc.nc
     with ExitStack() as ctx:
         keep = ctx.enter_context(tc.tile_pool(name="keep", bufs=1))
+        reuse = ctx.enter_context(tc.tile_pool(name="reuse", bufs=1))
         psum = ctx.enter_context(tc.psum_pool(name="psum", bufs=1))
 
         def f32(name, width=S):
             return keep.tile([P, width], F32, name=name, tag=name, align_bytes=64)
+
+        def placed(name, dtype, shape, offset):
+            return reuse.tile([P, *shape], dtype, name=name, align_bytes=64, offset=offset)
 
         halves = [slice(h * HALF, (h + 1) * HALF) for h in range(2)]
 
@@ -41,103 +45,119 @@ def tile_picked_ycms2_share_p_kernel(
         word_table = [keep.tile([P, T], I32, name=f"word_table{g}", align_bytes=64) for g in range(PASSES)]
         lists = [keep.tile([P, S // 16], U16, name=f"list{i}") for i in range(4)]
         counters = [f32(f"counters{i}", U) for i in range(3)]
-        w_raw = keep.tile([P, PASSES, 4, N], F32, name="w_raw", align_bytes=64)
+        w_raw = [keep.tile([P, 4, N], F32, name="w_raw0", align_bytes=64), placed("w_raw1", F32, [4, N], 1024)]
 
         def load_words(g):
             nc.sync.dma_start(word_table[g][:], x_words[g].rearrange("p c r -> p (c r)").bitcast(I32))
 
-        load_words(0)
+        def load_weights(g):
+            nc.sync.dma_start(w_raw[g][:], w1[512 * g : 512 * (g + 1), :].rearrange("(p j) n -> p j n", j=4))
+
         nc.sync.dma_start(lists[0][:], offs)
+        load_words(0)
         for q in range(4):
             nc.sync.dma_start(
                 scale_table[32 * q : 32 * q + 8, :].bitcast(I32),
                 x_scales[:, 4 * q : 4 * q + 4, :].bitcast(I32),
             )
-        nc.sync.dma_start(w_raw[:], w1.rearrange("(g p j) n -> p g j n", g=PASSES, j=4))
+        load_weights(0)
+        load_weights(1)
         load_words(1)
         for i, (table, hashes) in enumerate(((cnt0, hash0), (cnt1, hash1), (cnt2, hash2))):
-            nc.sync.dma_start(lists[1 + i][:], hashes)
             nc.sync.dma_start(counters[i][:], table)
+            nc.sync.dma_start(lists[1 + i][:], hashes)
 
-        w_bf = [keep.tile([P, N, 4], BF16, name=f"w_bf{g}", tag=f"w_bf{g}", align_bytes=64) for g in range(PASSES)]
+        w_bf = [keep.tile([P, N, 4], BF16, name=f"w_bf{g}", align_bytes=64) for g in range(PASSES)]
         for g in range(PASSES):
-            nc.scalar.activation(w_bf[g][:], w_raw[:, g].rearrange("p j n -> p n j"), ACT.Copy)
-
-        words0 = keep.tile([P, S], U32, name="words0", align_bytes=64)
-        nc.vector.tensor_copy(words0[:], word_table[0][:].bitcast(U32).indirect(lists[0][:]))
-        scales = keep.tile([P, S], U8, name="scales", align_bytes=64)
-        nc.vector.tensor_copy(scales[:], scale_table[:].indirect(lists[0][:]))
+            nc.scalar.activation(w_bf[g][:], w_raw[g][:].rearrange("p j n -> p n j"), ACT.Copy)
 
         w_codes = keep.tile([P, PASSES * N], U32, name="w_codes", align_bytes=64)
         w_scales = keep.tile([P, PASSES * N], U8, name="w_scales", align_bytes=64)
-        words1 = []
-        for g in range(PASSES):
+
+        def quantise(g):
             nc.vector.quantize_mx(
                 out=w_codes[:, g * N : (g + 1) * N].bitcast(FP8X4),
                 scales=w_scales[:, g * N : (g + 1) * N],
                 in_=w_bf[g][:].rearrange("p n j -> p (n j)"),
             )
-            words1.append(keep.tile([P, HALF], U32, name=f"words1_{g}", tag=f"w_bf{g}", align_bytes=64))
+
+        words = [keep.tile([P, S], U32, name="words0", align_bytes=64), placed("words1", U32, [S], 0)]
+        scales = keep.tile([P, S], U8, name="scales", align_bytes=64)
+        nc.vector.tensor_copy(words[0][:], word_table[0][:].bitcast(U32).indirect(lists[0][:]))
+        nc.vector.tensor_copy(scales[:], scale_table[:].indirect(lists[0][:]))
+        quantise(0)
+        quantise(1)
+        for h in range(2):
             nc.vector.tensor_copy(
-                words1[g][:], word_table[1][:].bitcast(U32).indirect(lists[0][:, 16 * g : 16 * (g + 1)])
+                words[1][:, halves[h]], word_table[1][:].bitcast(U32).indirect(lists[0][:, 16 * h : 16 * (h + 1)])
             )
 
         y = [psum.tile([P, HALF], F32, name=f"y{h}") for h in range(2)]
         for g in range(PASSES):
             for h in range(2):
-                moving = words0[:, halves[h]] if g == 0 else words1[h][:]
                 nc.tensor.matmul_mx(
                     out=y[h][:],
                     lhsT=w_codes[:, g * N : (g + 1) * N].bitcast(FP8X4),
                     lhsT_scale=w_scales[:, g * N : (g + 1) * N],
-                    rhs=moving.bitcast(FP8X4),
+                    rhs=words[g][:, halves[h]].bitcast(FP8X4),
                     rhs_scale=scales[4 * g : P, halves[h]],
                     start=(g == 0),
                     stop=(g == PASSES - 1),
                 )
 
-        y_abs = f32("y_abs")
+        y_abs = placed("y_abs", F32, [S], 8192)
         decay = f32("decay")
         for h in range(2):
             nc.scalar.activation(y_abs[:, halves[h]], y[h][:], ACT.Abs)
             nc.scalar.activation(decay[:, halves[h]], y_abs[:, halves[h]], ACT.Exp, scale=-1.0)
-        log1p = f32("log1p")
+        log1p = placed("log1p", F32, [S], 8192 - 1024)
         for h in range(2):
             nc.scalar.activation(log1p[:, halves[h]], decay[:, halves[h]], ACT.Ln, bias=1.0)
 
-        picked = [f32(f"picked{i}") for i in range(3)]
-        for i in range(3):
+        picked01 = placed("picked01", F32, [2 * S], 2048)
+        picked = [picked01[:, :S], picked01[:, S:], f32("picked2")]
+        for i in range(2):
             nc.vector.tensor_copy(picked[i][:], counters[i][:].indirect(lists[1 + i][:]))
+        for h in range(2):
+            nc.vector.tensor_copy(
+                picked[2][:, halves[h]], counters[2][:].indirect(lists[3][:, 16 * h : 16 * (h + 1)])
+            )
 
-        late = keep.tile([P, 3 * S], F32, name="late", tag="counters2", align_bytes=64)
-        low01, inc, high01 = (late[:, i * S : (i + 1) * S] for i in range(3))
-        low, high = f32("low"), f32("high")
-        nc.vector.tensor_tensor(low01[:], picked[0][:], picked[1][:], ALU.min)
+        low02, low, high02 = f32("low02"), f32("low"), f32("high02")
+        inc = keep.tile([P, S], F32, name="inc", tag="counters2", align_bytes=64)
+        for h in range(2):
+            nc.vector.tensor_tensor(low02[:, halves[h]], picked[0][:, halves[h]], picked[2][:, halves[h]], ALU.min)
         for h in range(2):
             nc.vector.scalar_tensor_tensor(
                 inc[:, halves[h]], y[h][:], 0.0, log1p[:, halves[h]], ALU.max, ALU.add
             )
-        nc.vector.tensor_tensor(low[:], low01[:], picked[2][:], ALU.min)
+        nc.vector.tensor_tensor(low[:], low02[:], picked[1][:], ALU.min)
         for h in range(2):
-            nc.vector.tensor_tensor(high01[:, halves[h]], picked[0][:, halves[h]], picked[1][:, halves[h]], ALU.max)
-        for h in range(2):
-            nc.vector.tensor_tensor(high[:, halves[h]], high01[:, halves[h]], picked[2][:, halves[h]], ALU.max)
+            nc.vector.tensor_tensor(high02[:, halves[h]], picked[0][:, halves[h]], picked[2][:, halves[h]], ALU.max)
 
-        ln_inc, ln_low, ln_low2, ln_high2 = (f32(n) for n in ("ln_inc", "ln_low", "ln_low2", "ln_high2"))
+        ln_mid = placed("ln_mid", F32, [S], 8192 + 1024)
+        ln_low02, ln_inc, ln_low, ln_high02 = (f32(n) for n in ("ln_low02", "ln_inc", "ln_low", "ln_high02"))
+        nc.scalar.activation(ln_mid[:], picked[1][:], ACT.Ln, bias=0.2)
+        nc.scalar.activation(ln_low02[:], low02[:], ACT.Ln, bias=0.2)
         nc.scalar.activation(ln_inc[:], inc[:], ACT.Ln, bias=TINY_INC)
         nc.scalar.activation(ln_low[:], low[:], ACT.Ln, bias=TINY_MIN)
-        nc.scalar.activation(ln_low2[:], low[:], ACT.Ln, bias=0.2)
         for h in range(2):
-            nc.scalar.activation(ln_high2[:, halves[h]], high[:, halves[h]], ACT.Ln, bias=0.2)
+            nc.scalar.activation(ln_high02[:, halves[h]], high02[:, halves[h]], ACT.Ln, bias=0.2)
 
-        spread, share, result = (f32(n) for n in ("spread", "share", "result"))
-        logit = high
+        ln_bottom = keep.tile([P, S], F32, name="ln_bottom", tag="low02", align_bytes=64)
+        logit = keep.tile([P, S], F32, name="logit", tag="high02", align_bytes=64)
+        ln_top, spread, share, result = (f32(n) for n in ("ln_top", "spread", "share", "result"))
+        nc.vector.tensor_tensor(ln_bottom[:], ln_low02[:], ln_mid[:], ALU.min)
         nc.vector.tensor_tensor(logit[:], ln_inc[:], ln_low[:], ALU.subtract)
-        nc.vector.tensor_tensor(spread[:], ln_high2[:], ln_low2[:], ALU.subtract)
         for h in range(2):
-            nc.scalar.activation(share[:, halves[h]], logit[:, halves[h]], ACT.Sigmoid)
+            nc.vector.tensor_tensor(ln_top[:, halves[h]], ln_high02[:, halves[h]], ln_mid[:, halves[h]], ALU.max)
         for h in range(2):
-            nc.vector.scalar_tensor_tensor(
-                result[:, halves[h]], spread[:, halves[h]], 0.3, share[:, halves[h]], ALU.mult, ALU.add
+            nc.vector.tensor_tensor(
+                spread[:, halves[h]], ln_top[:, halves[h]], ln_bottom[:, halves[h]], ALU.subtract
             )
-            nc.sync.dma_start(out[:, halves[h]], result[:, halves[h]])
+        quarters = [slice(q * S // 4, (q + 1) * S // 4) for q in range(4)]
+        for cols in quarters:
+            nc.scalar.activation(share[:, cols], logit[:, cols], ACT.Sigmoid)
+        for cols in quarters:
+            nc.vector.scalar_tensor_tensor(result[:, cols], spread[:, cols], 0.3, share[:, cols], ALU.mult, ALU.add)
+            nc.sync.dma_start(out[:, cols], result[:, cols])

@@ -45,7 +45,7 @@ def tile_picked_ycms2_share_p_kernel(
         word_table = [keep.tile([P, T], I32, name=f"word_table{g}", align_bytes=64) for g in range(PASSES)]
         lists = [keep.tile([P, S // 16], U16, name=f"list{i}") for i in range(4)]
         counters = [f32(f"counters{i}", U) for i in range(3)]
-        w_raw = [keep.tile([P, 4, N], F32, name="w_raw0", align_bytes=64), placed("w_raw1", F32, [4, N], 1024)]
+        w_raw = [placed("w_raw0", F32, [4, N], 0), placed("w_raw1", F32, [4, N], 2048)]
 
         def load_words(g):
             nc.sync.dma_start(word_table[g][:], x_words[g].rearrange("p c r -> p (c r)").bitcast(I32))
@@ -53,16 +53,16 @@ def tile_picked_ycms2_share_p_kernel(
         def load_weights(g):
             nc.sync.dma_start(w_raw[g][:], w1[512 * g : 512 * (g + 1), :].rearrange("(p j) n -> p j n", j=4))
 
-        nc.sync.dma_start(lists[0][:], offs)
         load_words(0)
+        nc.sync.dma_start(lists[0][:], offs)
         for q in range(4):
             nc.sync.dma_start(
                 scale_table[32 * q : 32 * q + 8, :].bitcast(I32),
                 x_scales[:, 4 * q : 4 * q + 4, :].bitcast(I32),
             )
         load_weights(0)
-        load_weights(1)
         load_words(1)
+        load_weights(1)
         for i, (table, hashes) in enumerate(((cnt0, hash0), (cnt1, hash1), (cnt2, hash2))):
             nc.sync.dma_start(counters[i][:], table)
             nc.sync.dma_start(lists[1 + i][:], hashes)
@@ -86,11 +86,8 @@ def tile_picked_ycms2_share_p_kernel(
         nc.vector.tensor_copy(words[0][:], word_table[0][:].bitcast(U32).indirect(lists[0][:]))
         nc.vector.tensor_copy(scales[:], scale_table[:].indirect(lists[0][:]))
         quantise(0)
+        nc.vector.tensor_copy(words[1][:], word_table[1][:].bitcast(U32).indirect(lists[0][:]))
         quantise(1)
-        for h in range(2):
-            nc.vector.tensor_copy(
-                words[1][:, halves[h]], word_table[1][:].bitcast(U32).indirect(lists[0][:, 16 * h : 16 * (h + 1)])
-            )
 
         y = [psum.tile([P, HALF], F32, name=f"y{h}") for h in range(2)]
         for g in range(PASSES):
@@ -109,6 +106,7 @@ def tile_picked_ycms2_share_p_kernel(
         decay = f32("decay")
         for h in range(2):
             nc.scalar.activation(y_abs[:, halves[h]], y[h][:], ACT.Abs)
+        for h in range(2):
             nc.scalar.activation(decay[:, halves[h]], y_abs[:, halves[h]], ACT.Exp, scale=-1.0)
         log1p = placed("log1p", F32, [S], 8192 - 1024)
         for h in range(2):

from contextlib import ExitStack

import concourse.mybir as mybir

K, T, S, N, U = 1024, 1024, 512, 128, 1024
FLOPS = 2 * K * S * N

F32 = mybir.dt.float32
BF16 = mybir.dt.bfloat16
I32 = mybir.dt.int32
U32 = mybir.dt.uint32
U16 = mybir.dt.uint16
U8 = mybir.dt.uint8
FP8X4 = mybir.dt.float8_e4m3fn_x4
ALU = mybir.AluOpType
ACT = mybir.ActivationFunctionType

P = 128
PASSES = 2
HALF = S // 2
TINY_INC = 2.0 ** -44
TINY_MIN = 2.0 ** -63


def tile_picked_ycms2_share_p_kernel(
    tc, x_words, x_scales, w1, cnt0, cnt1, cnt2, offs, hash0, hash1, hash2, out
):
    nc = tc.nc
    with ExitStack() as ctx:
        keep = ctx.enter_context(tc.tile_pool(name="keep", bufs=1))
        reuse = ctx.enter_context(tc.tile_pool(name="reuse", bufs=1))
        psum = ctx.enter_context(tc.psum_pool(name="psum", bufs=1))

        def f32(name, width=S):
            return keep.tile([P, width], F32, name=name, tag=name, align_bytes=64)

        def placed(name, dtype, shape, offset):
            return reuse.tile([P, *shape], dtype, name=name, align_bytes=64, offset=offset)

        halves = [slice(h * HALF, (h + 1) * HALF) for h in range(2)]

        scale_table = keep.tile([P, T], U8, name="scale_table", align_bytes=64)
        nc.vector.memset(scale_table[:].bitcast(I32), 0)

        word_table = [keep.tile([P, T], I32, name=f"word_table{g}", align_bytes=64) for g in range(PASSES)]
        lists = [keep.tile([P, S // 16], U16, name=f"list{i}") for i in range(4)]
        counters = [f32(f"counters{i}", U) for i in range(3)]
        w_raw = [placed("w_raw0", F32, [4, N], 0), placed("w_raw1", F32, [4, N], 2048)]

        def load_words(g):
            nc.sync.dma_start(word_table[g][:], x_words[g].rearrange("p c r -> p (c r)").bitcast(I32))

        def load_weights(g):
            nc.sync.dma_start(w_raw[g][:], w1[512 * g : 512 * (g + 1), :].rearrange("(p j) n -> p j n", j=4))

        load_words(0)
        nc.sync.dma_start(lists[0][:], offs)
        for q in range(4):
            nc.sync.dma_start(
                scale_table[32 * q : 32 * q + 8, :].bitcast(I32),
                x_scales[:, 4 * q : 4 * q + 4, :].bitcast(I32),
            )
        load_weights(0)
        load_words(1)
        load_weights(1)
        for i, (table, hashes) in enumerate(((cnt0, hash0), (cnt1, hash1), (cnt2, hash2))):
            nc.sync.dma_start(counters[i][:], table)
            nc.sync.dma_start(lists[1 + i][:], hashes)

        w_bf = [keep.tile([P, N, 4], BF16, name=f"w_bf{g}", align_bytes=64) for g in range(PASSES)]
        for g in range(PASSES):
            nc.scalar.activation(w_bf[g][:], w_raw[g][:].rearrange("p j n -> p n j"), ACT.Copy)

        w_codes = keep.tile([P, PASSES * N], U32, name="w_codes", align_bytes=64)
        w_scales = keep.tile([P, PASSES * N], U8, name="w_scales", align_bytes=64)

        def quantise(g):
            nc.vector.quantize_mx(
                out=w_codes[:, g * N : (g + 1) * N].bitcast(FP8X4),
                scales=w_scales[:, g * N : (g + 1) * N],
                in_=w_bf[g][:].rearrange("p n j -> p (n j)"),
            )

        words = [keep.tile([P, S], U32, name="words0", align_bytes=64), placed("words1", U32, [S], 0)]
        scales = keep.tile([P, S], U8, name="scales", align_bytes=64)
        nc.vector.tensor_copy(words[0][:], word_table[0][:].bitcast(U32).indirect(lists[0][:]))
        nc.vector.tensor_copy(scales[:], scale_table[:].indirect(lists[0][:]))
        quantise(0)
        nc.vector.tensor_copy(words[1][:], word_table[1][:].bitcast(U32).indirect(lists[0][:]))
        quantise(1)

        y = [psum.tile([P, HALF], F32, name=f"y{h}") for h in range(2)]
        for g in range(PASSES):
            for h in range(2):
                nc.tensor.matmul_mx(
                    out=y[h][:],
                    lhsT=w_codes[:, g * N : (g + 1) * N].bitcast(FP8X4),
                    lhsT_scale=w_scales[:, g * N : (g + 1) * N],
                    rhs=words[g][:, halves[h]].bitcast(FP8X4),
                    rhs_scale=scales[4 * g : P, halves[h]],
                    start=(g == 0),
                    stop=(g == PASSES - 1),
                )

        y_abs = placed("y_abs", F32, [S], 8192)
        decay = f32("decay")
        for h in range(2):
            nc.scalar.activation(y_abs[:, halves[h]], y[h][:], ACT.Abs)
        for h in range(2):
            nc.scalar.activation(decay[:, halves[h]], y_abs[:, halves[h]], ACT.Exp, scale=-1.0)
        log1p = placed("log1p", F32, [S], 8192 - 1024)
        for h in range(2):
            nc.scalar.activation(log1p[:, halves[h]], decay[:, halves[h]], ACT.Ln, bias=1.0)

        picked01 = placed("picked01", F32, [2 * S], 2048)
        picked = [picked01[:, :S], picked01[:, S:], f32("picked2")]
        for i in range(2):
            nc.vector.tensor_copy(picked[i][:], counters[i][:].indirect(lists[1 + i][:]))
        for h in range(2):
            nc.vector.tensor_copy(
                picked[2][:, halves[h]], counters[2][:].indirect(lists[3][:, 16 * h : 16 * (h + 1)])
            )

        low02, low, high02 = f32("low02"), f32("low"), f32("high02")
        inc = keep.tile([P, S], F32, name="inc", tag="counters2", align_bytes=64)
        for h in range(2):
            nc.vector.tensor_tensor(low02[:, halves[h]], picked[0][:, halves[h]], picked[2][:, halves[h]], ALU.min)
        for h in range(2):
            nc.vector.scalar_tensor_tensor(
                inc[:, halves[h]], y[h][:], 0.0, log1p[:, halves[h]], ALU.max, ALU.add
            )
        nc.vector.tensor_tensor(low[:], low02[:], picked[1][:], ALU.min)
        for h in range(2):
            nc.vector.tensor_tensor(high02[:, halves[h]], picked[0][:, halves[h]], picked[2][:, halves[h]], ALU.max)

        ln_mid = placed("ln_mid", F32, [S], 8192 + 1024)
        ln_low02, ln_inc, ln_low, ln_high02 = (f32(n) for n in ("ln_low02", "ln_inc", "ln_low", "ln_high02"))
        nc.scalar.activation(ln_mid[:], picked[1][:], ACT.Ln, bias=0.2)
        nc.scalar.activation(ln_low02[:], low02[:], ACT.Ln, bias=0.2)
        nc.scalar.activation(ln_inc[:], inc[:], ACT.Ln, bias=TINY_INC)
        nc.scalar.activation(ln_low[:], low[:], ACT.Ln, bias=TINY_MIN)
        for h in range(2):
            nc.scalar.activation(ln_high02[:, halves[h]], high02[:, halves[h]], ACT.Ln, bias=0.2)

        ln_bottom = keep.tile([P, S], F32, name="ln_bottom", tag="low02", align_bytes=64)
        logit = keep.tile([P, S], F32, name="logit", tag="high02", align_bytes=64)
        ln_top, spread, share, result = (f32(n) for n in ("ln_top", "spread", "share", "result"))
        nc.vector.tensor_tensor(ln_bottom[:], ln_low02[:], ln_mid[:], ALU.min)
        nc.vector.tensor_tensor(logit[:], ln_inc[:], ln_low[:], ALU.subtract)
        for h in range(2):
            nc.vector.tensor_tensor(ln_top[:, halves[h]], ln_high02[:, halves[h]], ln_mid[:, halves[h]], ALU.max)
        for h in range(2):
            nc.vector.tensor_tensor(
                spread[:, halves[h]], ln_top[:, halves[h]], ln_bottom[:, halves[h]], ALU.subtract
            )
        quarters = [slice(q * S // 4, (q + 1) * S // 4) for q in range(4)]
        for cols in quarters:
            nc.scalar.activation(share[:, cols], logit[:, cols], ACT.Sigmoid)
        for cols in quarters:
            nc.vector.scalar_tensor_tensor(result[:, cols], spread[:, cols], 0.3, share[:, cols], ALU.mult, ALU.add)
            nc.sync.dma_start(out[:, cols], result[:, cols])
